import numpy as np
import ml_dtypes


def mxq(x, axis, fmt="e4m3"):
    dtype, down = {"e4m3": (ml_dtypes.float8_e4m3fn, 7), "e5m2": (ml_dtypes.float8_e5m2, 14)}[fmt]
    v = np.moveaxis(np.asarray(x, np.float32).astype(ml_dtypes.bfloat16).astype(np.float64), axis, -1)
    blocks = v.reshape(v.shape[:-1] + (-1, 32))
    amax = np.abs(blocks).max(-1, keepdims=True)
    byte = np.maximum(np.where(amax > 0, np.frexp(amax)[1] - 1 + 127, 0) - down, 1)
    scale = np.exp2(byte - 127.0)
    codes = (blocks / scale).astype(np.float32).astype(dtype).astype(np.float64)
    return np.moveaxis((codes * scale).reshape(v.shape), -1, axis)


WIDE = False


def mx_kscale(k):
    if not WIDE:
        return np.ones(k)
    levels = np.array([10, -10, 5, -5, 0])
    if k % 512:
        return np.exp2(np.random.permutation(np.resize(levels, k // 32))).repeat(32)
    a = np.empty((k // 512, 16))
    for p in range(k // 512):
        a[p, :8] = np.random.permutation(np.resize(levels, 8))
        for g in range(8):
            far = levels[np.abs(levels - a[p, g]) >= 10]
            a[p, g + 8] = far[np.random.randint(len(far))]
    return np.exp2(a.ravel()).repeat(32)


BF16 = ml_dtypes.bfloat16


def bf(x):
    return np.asarray(x, np.float32).astype(BF16)


def f64(x):
    return np.asarray(x).astype(np.float64)


E2M1 = np.array([0.0, 0.5, 1.0, 1.5, 2.0, 3.0, 4.0, 6.0, -0.0, -0.5, -1.0, -1.5, -2.0, -3.0, -4.0, -6.0])


def pack_weight(w, fmt):
    k, n = w.shape
    w = f64(bf(w)).reshape(k // 32, 32, n)
    amax = np.abs(w).max(1)
    if fmt == "e4m3":
        byte = np.frexp(amax)[1] - 1 + 127 - 7
    else:
        mant, ex = np.frexp(amax / 6.0)
        byte = np.where(mant > 0.5, ex, ex - 1) + 127
    byte = np.clip(np.where(amax > 0, byte, 1), 1, 254)
    scaled = (w * np.exp2(127.0 - byte)[:, None, :]).reshape(k, n).astype(np.float32)
    by_word = np.ascontiguousarray(scaled.reshape(k // 512, 128, 4, n).transpose(0, 1, 3, 2))
    if fmt == "e4m3":
        words = by_word.astype(ml_dtypes.float8_e4m3fn).view(np.uint8)
    else:
        c = by_word.astype(ml_dtypes.float4_e2m1fn).view(np.uint8) & 0xF
        words = c[..., 0::2] | (c[..., 1::2] << 4)
    return np.ascontiguousarray(words), np.ascontiguousarray(byte.astype(np.uint8).reshape(k // 512, 16, n))


def unpack_weight(words, scales, fmt):
    g, p, n, _ = words.shape
    if fmt == "e4m3":
        vals = np.ascontiguousarray(words).view(ml_dtypes.float8_e4m3fn).astype(np.float64)
    else:
        nib = np.empty((g, p, n, 4), np.uint8)
        nib[..., 0::2] = words & 0xF
        nib[..., 1::2] = words >> 4
        vals = E2M1[nib]
    vals = vals * np.repeat(np.exp2(scales.astype(np.float64) - 127.0), 8, axis=1)[..., None]
    return vals.transpose(0, 1, 3, 2).reshape(g * 512, n)
def pack4(w):
    words, scales = pack_weight(w, "e2m1")
    return words.reshape(words.shape[0], 128, -1), scales


def unpack4(words, scales):
    return unpack_weight(words.reshape(words.shape[0], 128, -1, 2), scales, "e2m1")


E4M3FN = np.array([(-1.0 if i & 128 else 1.0) * ((1.0 + (i & 7) / 8.0) * 2.0 ** (((i >> 3) & 15) - 7) if i & 120 else (i & 7) * 2.0 ** -9) for i in range(256)])


def e4m3fn_bytes(y):
    return np.clip(np.asarray(y, np.float64), -448.0, 448.0).astype(np.float32).astype(ml_dtypes.float8_e4m3fn).view(np.uint8)


def e4m3fn_values(b):
    return E4M3FN[b]


T, K, C, D, B = 2048, 1536, 1024, 512, 128


def setup_inputs():
    s = mx_kscale(K)
    x = np.random.standard_normal((T, K)) * s
    x_scale = (np.abs(x).reshape(T, K // B, B).max(axis=2) / 448.0).astype(np.float32)
    x_bytes = e4m3fn_bytes(x / np.repeat(f64(x_scale), B, axis=1))
    v = np.random.standard_normal((K, D)) / np.sqrt(K) / s[:, None]
    v_words, v_scales = pack4(v)
    return {"x_bytes": x_bytes,
            "x_scale": x_scale,
            "w": bf(np.random.standard_normal((C, K)) / np.sqrt(K) / s),
            "b": bf(0.4 * np.random.standard_normal(C)),
            "m": bf(np.random.uniform(0.4, 1.0, T)),
            "v_words": v_words,
            "v_scales": v_scales,
            "c": bf(0.4 * np.random.standard_normal(D))}


def reference(x_bytes, x_scale, w, b, m, v_words, v_scales, c):
    x = e4m3fn_values(x_bytes) * np.repeat(f64(x_scale), B, axis=1)
    xq = mxq(x, 1, "e4m3")
    z = xq @ mxq(f64(w), 1, "e4m3").T
    concepts = (z + f64(b)) * f64(m)[:, None]
    d = xq @ unpack4(v_words, v_scales)
    depth = np.maximum(d + f64(c), 0.0)
    return concepts, depth

@@ -1,0 +1,307 @@
+from contextlib import ExitStack
+
+import concourse.mybir as mybir
+from concourse.masks import make_identity
+
+T, K, C, D = 2048, 1536, 1024, 512
+FLOPS = 2 * T * K * (C + D)
+
+F32 = mybir.dt.float32
+BF16 = mybir.dt.bfloat16
+I32 = mybir.dt.int32
+U32 = mybir.dt.uint32
+U8 = mybir.dt.uint8
+FP8 = mybir.dt.float8_e4m3fn
+FP8X4 = mybir.dt.float8_e4m3fn_x4
+FP4X4 = mybir.dt.float4_e2m1fn_x4
+ADD = mybir.AluOpType.add
+MULT = mybir.AluOpType.mult
+COPY = mybir.ActivationFunctionType.Copy
+RELU = mybir.ActivationFunctionType.Relu
+
+P = 128
+G = K // 512
+TILES = T // P
+PAIRS = TILES // 2
+BLOCKS = K // 128
+STRAIGHT = [(), (2,), (2,), (2,), (2,), (2,), (2,), (2,)]
+
+HEAD = """
+    TW:00 TW:01 WI:00 BI:2 XW:01s BI:0 BI:1 XB:2 WI:01 TX:00 XB:0 WI:02
+    TX:01 XB:1 XX:00s QW:01 XW:00v XX:01s TX:02 QX:00 XX:02s QX:01 WI:10 WI:12
+    TW:10 QX:02 TW:11 WI:11 BM:00 QW:00 M:002 XW:02v XW:10s XW:12v TX:10 XW:11s
+    TX:11 EP:002 TX:12 XX:10s QW:02 XX:11s QW:10 M:012 QX:10 XX:12s QX:11 TW:20
+    QW:11 BM:01 QX:12 QW:12 TW:21 EP:012 WI:22 WI:20 M:000 XW:20v XW:21s M:010
+    EP:000 RL:00 QW:20 TW:30 RL:01 QW:21 XW:22v BM:10 TW:31 WI:21 TX:20 XW:30s
+    QW:22 M:102 EP:010 XW:31s QW:30 XX:20s TX:21 XW:32v TX:22 XX:21s QW:31 QW:32
+    M:100 XX:22s QX:20 QX:21 BM:11 QX:22 M:001 EP:102 EP:100 M:011 WI:32 EP:001
+    M:101 EP:011 RL:10 WI:30 M:112 BM:20 EP:101 M:110 EP:112 BM:21 M:111 WI:31
+    RL:11 EP:110 EP:111
+"""
+
+
+def tile_archived_patch_probes_d1_kernel(
+    tc, x_bytes, x_scale, w, b, m, v_words, v_scales, c, concepts, depth
+):
+    nc = tc.nc
+
+    x_rows = x_bytes.rearrange("(p i) k -> p i k", i=TILES)
+    concept_rows = concepts.rearrange("(p i) n -> p i n", i=TILES)
+    depth_rows = depth.rearrange("(p i) n -> p i n", i=TILES)
+
+    with ExitStack() as ctx:
+        keep = ctx.enter_context(tc.tile_pool(name="keep", bufs=1))
+        work = ctx.enter_context(tc.tile_pool(name="work", bufs=4))
+        psum = ctx.enter_context(tc.psum_pool(name="psum", bufs=8))
+        ctx.enter_context(tc.manual_schedule())
+
+        bias_row = keep.tile([P, C + D], BF16, name="bias_row")
+        ones = keep.tile([P, P], BF16, name="ones")
+        ident = keep.tile([P, P], F32, name="ident")
+        bias = keep.tile([P, C + D], F32, name="bias")
+        m_raw = keep.tile([P, TILES], BF16, name="m_raw")
+        m_col = keep.tile([P, TILES], F32, name="m_col")
+        x_sc = keep.tile([P, TILES * BLOCKS], F32, name="x_sc")
+        v_code = keep.tile([P, G, 2 * D], U8, name="v_code", align_bytes=64)
+        v_plane = keep.tile([P, G, D], U8, name="v_plane", align_bytes=64)
+        w_in = [keep.tile([P, K], BF16, name="w_in%d" % j, tag="w_in%d" % j) for j in range(C // P)]
+        x8 = [keep.tile([P, 2, K], U8, name="x8_%d" % i, tag="x8_%d" % i) for i in range(PAIRS)]
+        w_code = [keep.tile([P, G, 512], U32, name="w_code%d" % h, tag="w_code%d" % h, align_bytes=64) for h in range(2)]
+        w_plane = [keep.tile([P, G, 512], U8, name="w_plane%d" % h, tag="w_plane%d" % h, align_bytes=64) for h in range(2)]
+        x_code = [keep.tile([P, G, 256], U32, name="x_code%d" % i, tag="x_code%d" % i, align_bytes=64) for i in range(PAIRS)]
+        x_plane = [keep.tile([P, G, 256], U8, name="x_plane%d" % i, tag="x_plane%d" % i, align_bytes=64) for i in range(PAIRS)]
+
+        def load_w(j):
+            nc.sync.dma_start(out=w_in[j][:], in_=w[P * j : P * (j + 1), :])
+
+        def load_x(i):
+            nc.sync.dma_start(out=x8[i][:], in_=x_rows[:, 2 * i : 2 * i + 2, :])
+
+        nc.vector.memset(bias_row[:], 0.0)
+        nc.gpsimd.memset(v_plane[:].rearrange("p g n -> p (g n)").bitcast(I32), 0)
+        make_identity(nc, ident[:])
+        nc.vector.memset(ones[:], 1.0)
+        load_w(0)
+        load_w(1)
+        nc.scalar.dma_start(out=bias_row[0:1, 0:C], in_=b.rearrange("(o n) -> o n", o=1))
+        nc.scalar.dma_start(out=bias_row[0:1, C : C + D], in_=c.rearrange("(o n) -> o n", o=1))
+        nc.scalar.dma_start(out=x_sc[:], in_=x_scale.rearrange("(p i) j -> p (i j)", i=TILES))
+        nc.scalar.dma_start(out=m_raw[:], in_=m.rearrange("(p i) -> p i", i=TILES))
+        load_x(0)
+        load_w(2)
+        nc.sync.dma_start(out=v_code[:].bitcast(I32), in_=v_words.rearrange("g p n -> p g n").bitcast(I32))
+        for q in range(4):
+            nc.gpsimd.dma_start(
+                out=v_plane[32 * q : 32 * q + 4, :, :].bitcast(I32),
+                in_=v_scales[:, 4 * q : 4 * q + 4, :].rearrange("g r n -> r g n").bitcast(I32),
+            )
+        load_w(3)
+        load_x(1)
+        for j in range(4, 8):
+            load_w(j)
+        for i in range(2, PAIRS):
+            load_x(i)
+
+        straight = STRAIGHT
+        banks = {}
+        grouped = {}
+        wide = {}
+
+        def spread_bias(s):
+            cols = slice(512 * s, 512 * (s + 1))
+            banks["b", s] = psum.tile([P, 512], F32, name="bank", tag="bank")
+            nc.tensor.matmul(banks["b", s][:], lhsT=ones[:], rhs=bias_row[:, cols], start=True, stop=True)
+
+        def copy_bias(s):
+            nc.scalar.copy(out=bias[:, 512 * s : 512 * (s + 1)], in_=banks["b", s][:])
+
+        def turn_w(jj, a):
+            words = w_in[2 * jj + a][:].bitcast(F32)
+            for g in range(G):
+                if a == 0:
+                    banks["w", jj, g] = psum.tile([P, 2, 256], F32, name="turned", tag="bank")
+                for u in range(2):
+                    nc.tensor.transpose(
+                        banks["w", jj, g][:, u, P * a : P * (a + 1)],
+                        words[:, 256 * g + u : 256 * (g + 1) : 2],
+                        ident[:],
+                    )
+
+        def copy_out(key, engine):
+            kind, i, g = key
+            if (kind, i) not in grouped:
+                grouped[kind, i] = work.tile([P, G, 1024], BF16, name="grouped", tag="grouped", align_bytes=64)
+            out = grouped[kind, i][:, g, :].bitcast(F32).rearrange("p (r u) -> p r u", u=2)
+            source = banks[key][:].rearrange("p u r -> p r u")
+            if engine == "v":
+                nc.vector.tensor_copy(out=out, in_=source)
+            else:
+                nc.scalar.copy(out=out, in_=source)
+
+        def quantize_w(jj, g):
+            h, cols = jj // 2, slice(256 * (jj % 2), 256 * (jj % 2) + 256)
+            nc.vector.quantize_mx(
+                out=w_code[h][:, g, cols].bitcast(FP8X4), scales=w_plane[h][:, g, cols], in_=grouped["w", jj][:, g, :]
+            )
+
+        def widen(i, a, j):
+            if i not in wide:
+                wide[i] = work.tile([P, 2, K], BF16, name="wide", tag="wide")
+            g, q = divmod(j, 4)
+            col = BLOCKS * (2 * i + a) + j
+            if g in straight[i]:
+                nc.scalar.activation(
+                    out=wide[i][:, a, P * j : P * (j + 1)],
+                    in_=x8[i][:, a, P * j : P * (j + 1)].bitcast(FP8),
+                    func=COPY,
+                    scale=x_sc[:, col : col + 1],
+                )
+                return
+            out = wide[i][:, a, 512 * g : 512 * (g + 1)].rearrange("p (u s e) -> p s u e", u=2, e=2)
+            nc.vector.tensor_scalar(
+                out=out[:, 32 * q : 32 * (q + 1), :, :],
+                in0=x8[i][:, a, P * j : P * (j + 1)].bitcast(FP8).rearrange("p (s u e) -> p s u e", u=2, e=2),
+                scalar1=x_sc[:, col : col + 1],
+                scalar2=None,
+                op0=MULT,
+            )
+
+        def turn_x(i, g):
+            bank = psum.tile([P, 2, 256], F32, name="turned", tag="bank")
+            for a in range(2):
+                words = wide[i][:, a, :].bitcast(F32)
+                for u in range(2):
+                    if g in straight[i]:
+                        picked = words[:, 256 * g + u : 256 * (g + 1) : 2]
+                    else:
+                        picked = words[:, 256 * g + P * u : 256 * g + P * (u + 1)]
+                    nc.tensor.transpose(bank[:, u, P * a : P * (a + 1)], picked, ident[:])
+            banks["x", i, g] = bank
+
+        def quantize_x(i, g):
+            nc.vector.quantize_mx(
+                out=x_code[i][:, g, :].bitcast(FP8X4), scales=x_plane[i][:, g, :], in_=grouped["x", i][:, g, :]
+            )
+
+        def multiply(i, a, part):
+            bank = psum.tile([P, 512], F32, name="bank", tag="bank")
+            tokens = slice(P * a, P * (a + 1))
+            for g in range(G):
+                if part == 2:
+                    rhs, rhs_scale = v_code[:, g, :].bitcast(FP4X4), v_plane[:, g, :]
+                else:
+                    rhs, rhs_scale = w_code[part][:, g, :].bitcast(FP8X4), w_plane[part][:, g, :]
+                nc.tensor.matmul_mx(
+                    out=bank[:],
+                    lhsT=x_code[i][:, g, tokens].bitcast(FP8X4),
+                    lhsT_scale=x_plane[i][:, g, tokens],
+                    rhs=rhs,
+                    rhs_scale=rhs_scale,
+                    start=(g == 0),
+                    stop=(g == G - 1),
+                )
+            banks["m", i, a, part] = bank
+
+        con = {}
+        dep = {}
+
+        def scaled_bias(i, a):
+            if a == 0:
+                con[i] = work.tile([P, 2, C], F32, name="con", tag="con")
+            t = 2 * i + a
+            nc.scalar.activation(out=con[i][:, a, :], in_=bias[:, 0:C], func=COPY, scale=m_col[:, t : t + 1])
+
+        def finish_concepts(i, a, h):
+            t = 2 * i + a
+            place = con[i][:, a, 512 * h : 512 * (h + 1)]
+            nc.vector.scalar_tensor_tensor(
+                out=place, in0=banks["m", i, a, h][:], scalar=m_col[:, t : t + 1], in1=place, op0=MULT, op1=ADD
+            )
+
+        def add_depth(i, a):
+            if a == 0:
+                dep[i] = work.tile([P, 2, D], F32, name="dep", tag="dep")
+            nc.vector.tensor_tensor(out=dep[i][:, a, :], in0=banks["m", i, a, 2][:], in1=bias[:, C : C + D], op=ADD)
+
+        def relu_depth(i, a):
+            nc.scalar.activation(out=dep[i][:, a, :], in_=dep[i][:, a, :], func=RELU)
+
+        def store_concepts(i, a):
+            t = 2 * i + a
+            nc.sync.dma_start(out=concept_rows[:, t, :], in_=con[i][:, a, :])
+
+        def store_half(i, a, h):
+            t = 2 * i + a
+            cols = slice(512 * h, 512 * (h + 1))
+            nc.sync.dma_start(out=concept_rows[:, t, cols], in_=con[i][:, a, cols])
+
+        def store_depth(i):
+            nc.sync.dma_start(out=depth_rows[:, 2 * i : 2 * i + 2, :], in_=dep[i][:])
+
+        nc.vector.tensor_copy(out=m_col[:], in_=m_raw[:])
+
+        def widen_group(i, g):
+            for n in range(8):
+                widen(i, n // 4, 4 * g + n % 4)
+
+        def finish(i, a, part):
+            if part == 2:
+                add_depth(i, a)
+            else:
+                finish_concepts(i, a, part)
+                if i == PAIRS - 1:
+                    store_half(i, a, part)
+                elif part == 1:
+                    store_concepts(i, a)
+
+        def relu(i, a):
+            relu_depth(i, a)
+            if a == 1:
+                store_depth(i)
+
+        steps = {
+            "TW": turn_w,
+            "QW": quantize_w,
+            "BI": spread_bias,
+            "XB": copy_bias,
+            "WI": widen_group,
+            "TX": turn_x,
+            "QX": quantize_x,
+            "BM": scaled_bias,
+            "M": multiply,
+            "EP": finish,
+            "RL": relu,
+        }
+
+        for word in HEAD.split():
+            kind, digits = word.split(":")
+            if kind == "XW":
+                copy_out(("w", int(digits[0]), int(digits[1])), digits[2])
+            elif kind == "XX":
+                copy_out(("x", int(digits[0]), int(digits[1])), digits[2])
+            else:
+                steps[kind](*[int(n) for n in digits])
+
+        for i in range(2, PAIRS):
+            ahead = i + 1 < PAIRS
+            further = i + 2 < PAIRS
+            if further:
+                widen_group(i + 2, 2)
+            if ahead:
+                for g in range(G):
+                    turn_x(i + 1, g)
+                    copy_out(("x", i + 1, g), "s")
+            if further:
+                widen_group(i + 2, 0)
+                widen_group(i + 2, 1)
+            if ahead:
+                for g in range(G):
+                    quantize_x(i + 1, g)
+            for a in range(2):
+                if ahead:
+                    scaled_bias(i + 1, a)
+                for part in (2, 0, 1):
+                    multiply(i, a, part)
+                    finish(i, a, part)
+                    if part == 2:
+                        relu(i, a)

@@ -29,7 +29,7 @@ STRAIGHT = [(), (2,), (2,), (2,), (2,), (2,), (2,), (2,)]
 HEAD = """
     TW:00 TW:01 WI:00 BI:2 XW:01s BI:0 BI:1 XB:2 WI:01 TX:00 XB:0 WI:02
     TX:01 XB:1 XX:00s QW:01 XW:00v XX:01s TX:02 QX:00 XX:02s QX:01 WI:10 WI:12
-    TW:10 QX:02 TW:11 WI:11 BM:00 QW:00 M:002 XW:02v XW:10s XW:12v TX:10 XW:11s
+    TW:10 QX:02 TW:11 MC:0 WI:11 BM:00 QW:00 M:002 XW:02v XW:10s XW:12v TX:10 XW:11s
     TX:11 EP:002 TX:12 XX:10s QW:02 XX:11s QW:10 M:012 QX:10 XX:12s QX:11 TW:20
     QW:11 BM:01 QX:12 QW:12 TW:21 EP:012 WI:22 WI:20 M:000 XW:20v XW:21s M:010
     EP:000 RL:00 QW:20 TW:30 RL:01 QW:21 XW:22v BM:10 TW:31 WI:21 TX:20 XW:30s
@@ -78,10 +78,11 @@ def tile_archived_patch_probes_d1_kernel(
             nc.sync.dma_start(out=x8[i][:], in_=x_rows[:, 2 * i : 2 * i + 2, :])
 
         nc.vector.memset(bias_row[:], 0.0)
-        nc.gpsimd.memset(v_plane[:].rearrange("p g n -> p (g n)").bitcast(I32), 0)
         make_identity(nc, ident[:])
         nc.vector.memset(ones[:], 1.0)
-        load_w(0)
+        nc.vector.memset(v_plane[:].rearrange("p g n -> p (g n)").bitcast(I32), 0)
+        for g in range(G):
+            nc.sync.dma_start(out=w_in[0][:, 512 * g : 512 * (g + 1)], in_=w[0:P, 512 * g : 512 * (g + 1)])
         load_w(1)
         nc.scalar.dma_start(out=bias_row[0:1, 0:C], in_=b.rearrange("(o n) -> o n", o=1))
         nc.scalar.dma_start(out=bias_row[0:1, C : C + D], in_=c.rearrange("(o n) -> o n", o=1))
@@ -91,7 +92,7 @@ def tile_archived_patch_probes_d1_kernel(
         load_w(2)
         nc.sync.dma_start(out=v_code[:].bitcast(I32), in_=v_words.rearrange("g p n -> p g n").bitcast(I32))
         for q in range(4):
-            nc.gpsimd.dma_start(
+            nc.sync.dma_start(
                 out=v_plane[32 * q : 32 * q + 4, :, :].bitcast(I32),
                 in_=v_scales[:, 4 * q : 4 * q + 4, :].rearrange("g r n -> r g n").bitcast(I32),
             )
@@ -183,24 +184,30 @@ def tile_archived_patch_probes_d1_kernel(
                 out=x_code[i][:, g, :].bitcast(FP8X4), scales=x_plane[i][:, g, :], in_=grouped["x", i][:, g, :]
             )
 
+        def pieces(i, a, part):
+            if (i, a, part) == (PAIRS - 1, 1, 1):
+                return [slice(0, 256), slice(256, 512)]
+            return [slice(0, 512)]
+
         def multiply(i, a, part):
-            bank = psum.tile([P, 512], F32, name="bank", tag="bank")
             tokens = slice(P * a, P * (a + 1))
-            for g in range(G):
-                if part == 2:
-                    rhs, rhs_scale = v_code[:, g, :].bitcast(FP4X4), v_plane[:, g, :]
-                else:
-                    rhs, rhs_scale = w_code[part][:, g, :].bitcast(FP8X4), w_plane[part][:, g, :]
-                nc.tensor.matmul_mx(
-                    out=bank[:],
-                    lhsT=x_code[i][:, g, tokens].bitcast(FP8X4),
-                    lhsT_scale=x_plane[i][:, g, tokens],
-                    rhs=rhs,
-                    rhs_scale=rhs_scale,
-                    start=(g == 0),
-                    stop=(g == G - 1),
-                )
-            banks["m", i, a, part] = bank
+            for cols in pieces(i, a, part):
+                bank = psum.tile([P, 512], F32, name="bank", tag="bank")
+                for g in range(G):
+                    if part == 2:
+                        rhs, rhs_scale = v_code[:, g, :].bitcast(FP4X4), v_plane[:, g, :]
+                    else:
+                        rhs, rhs_scale = w_code[part][:, g, cols].bitcast(FP8X4), w_plane[part][:, g, cols]
+                    nc.tensor.matmul_mx(
+                        out=bank[:, cols],
+                        lhsT=x_code[i][:, g, tokens].bitcast(FP8X4),
+                        lhsT_scale=x_plane[i][:, g, tokens],
+                        rhs=rhs,
+                        rhs_scale=rhs_scale,
+                        start=(g == 0),
+                        stop=(g == G - 1),
+                    )
+                banks["m", i, a, part, cols.start] = bank
 
         con = {}
         dep = {}
@@ -213,15 +220,24 @@ def tile_archived_patch_probes_d1_kernel(
 
         def finish_concepts(i, a, h):
             t = 2 * i + a
-            place = con[i][:, a, 512 * h : 512 * (h + 1)]
-            nc.vector.scalar_tensor_tensor(
-                out=place, in0=banks["m", i, a, h][:], scalar=m_col[:, t : t + 1], in1=place, op0=MULT, op1=ADD
-            )
+            for cols in pieces(i, a, h):
+                both = slice(512 * h + cols.start, 512 * h + cols.stop)
+                place = con[i][:, a, both]
+                nc.vector.scalar_tensor_tensor(
+                    out=place,
+                    in0=banks["m", i, a, h, cols.start][:, cols],
+                    scalar=m_col[:, t : t + 1],
+                    in1=place,
+                    op0=MULT,
+                    op1=ADD,
+                )
+                if i == PAIRS - 1:
+                    nc.sync.dma_start(out=concept_rows[:, t, both], in_=place)
 
         def add_depth(i, a):
             if a == 0:
                 dep[i] = work.tile([P, 2, D], F32, name="dep", tag="dep")
-            nc.vector.tensor_tensor(out=dep[i][:, a, :], in0=banks["m", i, a, 2][:], in1=bias[:, C : C + D], op=ADD)
+            nc.vector.tensor_tensor(out=dep[i][:, a, :], in0=banks["m", i, a, 2, 0][:], in1=bias[:, C : C + D], op=ADD)
 
         def relu_depth(i, a):
             nc.scalar.activation(out=dep[i][:, a, :], in_=dep[i][:, a, :], func=RELU)
@@ -230,15 +246,8 @@ def tile_archived_patch_probes_d1_kernel(
             t = 2 * i + a
             nc.sync.dma_start(out=concept_rows[:, t, :], in_=con[i][:, a, :])
 
-        def store_half(i, a, h):
-            t = 2 * i + a
-            cols = slice(512 * h, 512 * (h + 1))
-            nc.sync.dma_start(out=concept_rows[:, t, cols], in_=con[i][:, a, cols])
-
         def store_depth(i):
             nc.sync.dma_start(out=depth_rows[:, 2 * i : 2 * i + 2, :], in_=dep[i][:])
-
-        nc.vector.tensor_copy(out=m_col[:], in_=m_raw[:])
 
         def widen_group(i, g):
             for n in range(8):
@@ -249,9 +258,7 @@ def tile_archived_patch_probes_d1_kernel(
                 add_depth(i, a)
             else:
                 finish_concepts(i, a, part)
-                if i == PAIRS - 1:
-                    store_half(i, a, part)
-                elif part == 1:
+                if part == 1 and i < PAIRS - 1:
                     store_concepts(i, a)
 
         def relu(i, a):
@@ -275,7 +282,9 @@ def tile_archived_patch_probes_d1_kernel(
 
         for word in HEAD.split():
             kind, digits = word.split(":")
-            if kind == "XW":
+            if kind == "MC":
+                nc.vector.tensor_copy(out=m_col[:], in_=m_raw[:])
+            elif kind == "XW":
                 copy_out(("w", int(digits[0]), int(digits[1])), digits[2])
             elif kind == "XX":
                 copy_out(("x", int(digits[0]), int(digits[1])), digits[2])

@@ -15,6 +15,7 @@ FP8 = mybir.dt.float8_e4m3fn
 FP8X4 = mybir.dt.float8_e4m3fn_x4
 FP4X4 = mybir.dt.float4_e2m1fn_x4
 ADD = mybir.AluOpType.add
+MAX = mybir.AluOpType.max
 MULT = mybir.AluOpType.mult
 COPY = mybir.ActivationFunctionType.Copy
 RELU = mybir.ActivationFunctionType.Relu
@@ -24,20 +25,22 @@ G = K // 512
 TILES = T // P
 PAIRS = TILES // 2
 BLOCKS = K // 128
-STRAIGHT = [(), (2,), (2,), (2,), (2,), (2,), (2,), (2,)]
+STRAIGHT = [(2,), (2,), (2,), (2,), (2,), (2,), (2,), (2,)]
 
 HEAD = """
-    TW:00 TW:01 WI:00 BI:2 XW:01s BI:0 BI:1 XB:2 WI:01 TX:00 XB:0 WI:02
-    TX:01 XB:1 XX:00s QW:01 XW:00v XX:01s TX:02 QX:00 XX:02s QX:01 WI:10 WI:12
-    TW:10 QX:02 TW:11 MC:0 WI:11 BM:00 QW:00 M:002 XW:02v XW:10s XW:12v TX:10 XW:11s
-    TX:11 EP:002 TX:12 XX:10s QW:02 XX:11s QW:10 M:012 QX:10 XX:12s QX:11 TW:20
-    QW:11 BM:01 QX:12 QW:12 TW:21 EP:012 WI:22 WI:20 M:000 XW:20v XW:21s M:010
-    EP:000 RL:00 QW:20 TW:30 RL:01 QW:21 XW:22v BM:10 TW:31 WI:21 TX:20 XW:30s
-    QW:22 M:102 EP:010 XW:31s QW:30 XX:20s TX:21 XW:32v TX:22 XX:21s QW:31 QW:32
-    M:100 XX:22s QX:20 QX:21 BM:11 QX:22 M:001 EP:102 EP:100 M:011 WI:32 EP:001
-    M:101 EP:011 RL:10 WI:30 M:112 BM:20 EP:101 M:110 EP:112 BM:21 M:111 WI:31
-    RL:11 EP:110 EP:111
+    WI:00 WI:02 WI:01 TX:00 BI:2 XX:00s BI:0 TX:01 XB:0 QX:00 TX:02 XX:01s
+    TW:00 XX:02s WI:10 TW:01 XB:2 QX:02 WI:12 QX:01 TX:10 XW:00v BI:1 M:012
+    WI:11 MC:0 XW:01s M:002 XW:02s EP:012 XX:10s WI:21 TX:11 XB:1 TW:10 EP:002
+    XX:11s TX:12 QW:00 WI:22 WI:20 TW:20 QW:02 TW:11 QX:11 XX:12s QX:10 TW:21
+    XW:11s XW:10v QX:12 XW:12s TX:20 QW:11 TX:22 XX:20s QW:10 QW:12 TX:21 XX:22s
+    QW:01 M:102 XW:20s QX:22 WI:40 M:010 XW:22s XW:21s EP:102 M:112 XX:21s WI:30
+    M:100 BM:00 QX:21 QW:20 M:000 QW:22 BM:01 WI:31 TW:30 QX:20 BM:10 EP:010
+    TW:31 EP:112 M:202 XW:31s EP:100 XW:32s QW:21 M:110 EP:000 XW:30s M:212 BM:11
+    QW:30 QW:32 QW:31 M:200 WI:41 WI:42 M:210 EP:212 BM:20 EP:202 M:011 EP:110
+    M:111 WI:32 M:001 EP:111 BM:21 EP:200 M:211 EP:001 M:201 EP:210 EP:011 M:101
+    EP:211 EP:101 EP:201
 """
+GROUPS = ((3, 4), (5, 6, 7))
 
 
 def tile_archived_patch_probes_d1_kernel(
@@ -77,30 +80,34 @@ def tile_archived_patch_probes_d1_kernel(
         def load_x(i):
             nc.sync.dma_start(out=x8[i][:], in_=x_rows[:, 2 * i : 2 * i + 2, :])
 
+        warm = keep.tile([P, 512], BF16, name="warm")
+        nc.vector.memset(warm[:], 0.0)
         nc.vector.memset(bias_row[:], 0.0)
         make_identity(nc, ident[:])
         nc.vector.memset(ones[:], 1.0)
         nc.vector.memset(v_plane[:].rearrange("p g n -> p (g n)").bitcast(I32), 0)
-        for g in range(G):
-            nc.sync.dma_start(out=w_in[0][:, 512 * g : 512 * (g + 1)], in_=w[0:P, 512 * g : 512 * (g + 1)])
-        load_w(1)
+        nc.scalar.dma_start(out=x_sc[:], in_=x_scale.rearrange("(p i) j -> p (i j)", i=TILES))
+        load_x(0)
+        load_w(0)
         nc.scalar.dma_start(out=bias_row[0:1, 0:C], in_=b.rearrange("(o n) -> o n", o=1))
         nc.scalar.dma_start(out=bias_row[0:1, C : C + D], in_=c.rearrange("(o n) -> o n", o=1))
-        nc.scalar.dma_start(out=x_sc[:], in_=x_scale.rearrange("(p i) j -> p (i j)", i=TILES))
         nc.scalar.dma_start(out=m_raw[:], in_=m.rearrange("(p i) -> p i", i=TILES))
-        load_x(0)
-        load_w(2)
         nc.sync.dma_start(out=v_code[:].bitcast(I32), in_=v_words.rearrange("g p n -> p g n").bitcast(I32))
+        load_w(1)
         for q in range(4):
             nc.sync.dma_start(
                 out=v_plane[32 * q : 32 * q + 4, :, :].bitcast(I32),
                 in_=v_scales[:, 4 * q : 4 * q + 4, :].rearrange("g r n -> r g n").bitcast(I32),
             )
-        load_w(3)
         load_x(1)
-        for j in range(4, 8):
-            load_w(j)
-        for i in range(2, PAIRS):
+        load_w(2)
+        load_w(3)
+        load_w(4)
+        load_x(2)
+        load_w(5)
+        load_w(6)
+        load_w(7)
+        for i in range(3, PAIRS):
             load_x(i)
 
         straight = STRAIGHT
@@ -213,7 +220,7 @@ def tile_archived_patch_probes_d1_kernel(
         dep = {}
 
         def scaled_bias(i, a):
-            if a == 0:
+            if i not in con:
                 con[i] = work.tile([P, 2, C], F32, name="con", tag="con")
             t = 2 * i + a
             nc.scalar.activation(out=con[i][:, a, :], in_=bias[:, 0:C], func=COPY, scale=m_col[:, t : t + 1])
@@ -231,23 +238,20 @@ def tile_archived_patch_probes_d1_kernel(
                     op0=MULT,
                     op1=ADD,
                 )
-                if i == PAIRS - 1:
-                    nc.sync.dma_start(out=concept_rows[:, t, both], in_=place)
+                nc.sync.dma_start(out=concept_rows[:, t, both], in_=place)
 
         def add_depth(i, a):
-            if a == 0:
+            if i not in dep:
                 dep[i] = work.tile([P, 2, D], F32, name="dep", tag="dep")
             nc.vector.tensor_tensor(out=dep[i][:, a, :], in0=banks["m", i, a, 2, 0][:], in1=bias[:, C : C + D], op=ADD)
 
         def relu_depth(i, a):
-            nc.scalar.activation(out=dep[i][:, a, :], in_=dep[i][:, a, :], func=RELU)
-
-        def store_concepts(i, a):
-            t = 2 * i + a
-            nc.sync.dma_start(out=concept_rows[:, t, :], in_=con[i][:, a, :])
-
-        def store_depth(i):
-            nc.sync.dma_start(out=depth_rows[:, 2 * i : 2 * i + 2, :], in_=dep[i][:])
+            place = dep[i][:, a, :]
+            if i < PAIRS - 1:
+                nc.gpsimd.tensor_scalar(out=place, in0=place, scalar1=0.0, scalar2=0.0, op0=MAX, op1=ADD)
+            else:
+                nc.scalar.activation(out=place, in_=place, func=RELU)
+            nc.sync.dma_start(out=depth_rows[:, 2 * i + a, :], in_=place)
 
         def widen_group(i, g):
             for n in range(8):
@@ -256,15 +260,9 @@ def tile_archived_patch_probes_d1_kernel(
         def finish(i, a, part):
             if part == 2:
                 add_depth(i, a)
+                relu_depth(i, a)
             else:
                 finish_concepts(i, a, part)
-                if part == 1 and i < PAIRS - 1:
-                    store_concepts(i, a)
-
-        def relu(i, a):
-            relu_depth(i, a)
-            if a == 1:
-                store_depth(i)
 
         steps = {
             "TW": turn_w,
@@ -277,8 +275,11 @@ def tile_archived_patch_probes_d1_kernel(
             "BM": scaled_bias,
             "M": multiply,
             "EP": finish,
-            "RL": relu,
         }
+
+        for n in range(5):
+            spare = psum.tile([P, 512], F32, name="bank", tag="bank")
+            nc.tensor.matmul(spare[:], lhsT=warm[:, 0:P], rhs=warm[:], start=True, stop=True)
 
         for word in HEAD.split():
             kind, digits = word.split(":")
@@ -291,26 +292,28 @@ def tile_archived_patch_probes_d1_kernel(
             else:
                 steps[kind](*[int(n) for n in digits])
 
-        for i in range(2, PAIRS):
-            ahead = i + 1 < PAIRS
-            further = i + 2 < PAIRS
-            if further:
-                widen_group(i + 2, 2)
-            if ahead:
+        for n, group in enumerate(GROUPS):
+            coming = [(i, g) for i in (GROUPS[n + 1] if n + 1 < len(GROUPS) else ()) for g in range(G)]
+            for i in group:
                 for g in range(G):
-                    turn_x(i + 1, g)
-                    copy_out(("x", i + 1, g), "s")
-            if further:
-                widen_group(i + 2, 0)
-                widen_group(i + 2, 1)
-            if ahead:
+                    turn_x(i, g)
+                    copy_out(("x", i, g), "s")
+            done = 0
+            on_vector = [key for key in coming if key[1] not in straight[key[0]]]
+            on_scalar = [key for key in coming if key[1] in straight[key[0]]]
+            for i in group:
                 for g in range(G):
-                    quantize_x(i + 1, g)
-            for a in range(2):
-                if ahead:
-                    scaled_bias(i + 1, a)
-                for part in (2, 0, 1):
+                    quantize_x(i, g)
+            for i in group:
+                for a in range(2):
+                    scaled_bias(i, a)
+                for a, part in ((0, 2), (1, 2), (0, 0), (0, 1), (1, 0), (1, 1)):
                     multiply(i, a, part)
                     finish(i, a, part)
-                    if part == 2:
-                        relu(i, a)
+                    if part in (1, 2) and done < len(on_vector):
+                        widen_group(*on_vector[done])
+                        done += 1
+                for key in on_scalar[i - group[0] : i - group[0] + 1]:
+                    widen_group(*key)
+            for key in on_vector[done:] + on_scalar[len(group) :]:
+                widen_group(*key)

@@ -15,7 +15,6 @@ FP8 = mybir.dt.float8_e4m3fn
 FP8X4 = mybir.dt.float8_e4m3fn_x4
 FP4X4 = mybir.dt.float4_e2m1fn_x4
 ADD = mybir.AluOpType.add
-MAX = mybir.AluOpType.max
 MULT = mybir.AluOpType.mult
 COPY = mybir.ActivationFunctionType.Copy
 RELU = mybir.ActivationFunctionType.Relu
@@ -25,22 +24,25 @@ G = K // 512
 TILES = T // P
 PAIRS = TILES // 2
 BLOCKS = K // 128
-STRAIGHT = [(2,), (2,), (2,), (2,), (2,), (2,), (2,), (2,)]
+STRAIGHT = [(2,)] * 7 + [()]
 
 HEAD = """
-    WI:00 WI:02 WI:01 TX:00 BI:2 XX:00s BI:0 TX:01 XB:0 QX:00 TX:02 XX:01s
-    TW:00 XX:02s WI:10 TW:01 XB:2 QX:02 WI:12 QX:01 TX:10 XW:00v BI:1 M:012
-    WI:11 MC:0 XW:01s M:002 XW:02s EP:012 XX:10s WI:21 TX:11 XB:1 TW:10 EP:002
-    XX:11s TX:12 QW:00 WI:22 WI:20 TW:20 QW:02 TW:11 QX:11 XX:12s QX:10 TW:21
-    XW:11s XW:10v QX:12 XW:12s TX:20 QW:11 TX:22 XX:20s QW:10 QW:12 TX:21 XX:22s
-    QW:01 M:102 XW:20s QX:22 WI:40 M:010 XW:22s XW:21s EP:102 M:112 XX:21s WI:30
-    M:100 BM:00 QX:21 QW:20 M:000 QW:22 BM:01 WI:31 TW:30 QX:20 BM:10 EP:010
-    TW:31 EP:112 M:202 XW:31s EP:100 XW:32s QW:21 M:110 EP:000 XW:30s M:212 BM:11
-    QW:30 QW:32 QW:31 M:200 WI:41 WI:42 M:210 EP:212 BM:20 EP:202 M:011 EP:110
-    M:111 WI:32 M:001 EP:111 BM:21 EP:200 M:211 EP:001 M:201 EP:210 EP:011 M:101
-    EP:211 EP:101 EP:201
+    WI:00 WI:02 WI:01 TX:00 BI:1 XX:00s BI:2 XB:1 TX:01 QX:00 TX:02 XX:01s
+    TW:00 XX:02s WI:10 XB:2 TW:01 QX:01 WI:12 QX:02 TX:10 XW:01v BI:0 M:002
+    WI:11 MC:0 XX:10s XW:00s QW:01 M:012 EP:002 XB:0 QW:00 TX:12 XW:02s QX:10
+    WI:20 TX:11 BM:00 TW:10 EP:012 TW:11 XX:12s WI:21 XX:11s TW:20 QX:12 XW:11s
+    QW:02 TW:21 QX:11 XW:12s WI:31 XW:10s TX:20 QW:12 M:112 BM:01 QW:11 QW:10
+    WI:41 M:102 XW:20s XW:22v M:000 XX:20s EP:112 WI:22 M:110 EP:000 XW:21v M:010
+    BM:11 EP:102 TX:21 QW:21 TX:22 BM:10 WI:40 TW:30 EP:110 XX:21s TW:31 QX:20
+    XX:22s EP:010 M:100 XW:31s QX:21 QX:22 XW:32s QW:20 M:212 QW:31 XW:30s EP:100
+    M:202 RL:00 WI:51 BM:20 M:210 QW:32 QW:30 QW:22 M:200 WI:32 EP:212 EP:202
+    M:001 BM:21 WI:30 M:111 WI:61 RL:20 M:101 EP:001 RL:10 M:011 EP:210 WI:42
+    EP:111 TX:32 EP:200 RL:21 TX:41 EP:101 TX:30 XX:32s TX:31 WI:50 TX:40 XX:30s
+    TX:42 XX:31s EP:011 M:201 XX:40s QX:32 QX:30 XX:41s M:211 QX:31 WI:60 XX:42s
+    WI:52 EP:201 EP:211 QX:40 RL:01 QX:41 QX:42 RL:11 WI:62
 """
-GROUPS = ((3, 4), (5, 6, 7))
+TILE_ORDER = ((0, 2), (1, 2), (0, 0), (0, 1), (1, 0), (1, 1))
+GROUPS = ((3, 4), (5, 6), (7,))
 
 
 def tile_archived_patch_probes_d1_kernel(
@@ -80,8 +82,6 @@ def tile_archived_patch_probes_d1_kernel(
         def load_x(i):
             nc.sync.dma_start(out=x8[i][:], in_=x_rows[:, 2 * i : 2 * i + 2, :])
 
-        warm = keep.tile([P, 512], BF16, name="warm")
-        nc.vector.memset(warm[:], 0.0)
         nc.vector.memset(bias_row[:], 0.0)
         make_identity(nc, ident[:])
         nc.vector.memset(ones[:], 1.0)
@@ -216,6 +216,7 @@ def tile_archived_patch_probes_d1_kernel(
                     )
                 banks["m", i, a, part, cols.start] = bank
 
+        complete = set()
         con = {}
         dep = {}
 
@@ -238,7 +239,11 @@ def tile_archived_patch_probes_d1_kernel(
                     op0=MULT,
                     op1=ADD,
                 )
-                nc.sync.dma_start(out=concept_rows[:, t, both], in_=place)
+                if i == PAIRS - 1:
+                    nc.sync.dma_start(out=concept_rows[:, t, both], in_=place)
+            complete.add((i, a, h))
+            if (i, a, 1 - h) in complete and i < PAIRS - 1:
+                nc.sync.dma_start(out=concept_rows[:, t, :], in_=con[i][:, a, :])
 
         def add_depth(i, a):
             if i not in dep:
@@ -247,11 +252,12 @@ def tile_archived_patch_probes_d1_kernel(
 
         def relu_depth(i, a):
             place = dep[i][:, a, :]
-            if i < PAIRS - 1:
-                nc.gpsimd.tensor_scalar(out=place, in0=place, scalar1=0.0, scalar2=0.0, op0=MAX, op1=ADD)
-            else:
-                nc.scalar.activation(out=place, in_=place, func=RELU)
-            nc.sync.dma_start(out=depth_rows[:, 2 * i + a, :], in_=place)
+            nc.scalar.activation(out=place, in_=place, func=RELU)
+            complete.add((i, a))
+            if i == PAIRS - 1:
+                nc.sync.dma_start(out=depth_rows[:, 2 * i + a, :], in_=place)
+            elif (i, 1 - a) in complete:
+                nc.sync.dma_start(out=depth_rows[:, 2 * i : 2 * i + 2, :], in_=dep[i][:])
 
         def widen_group(i, g):
             for n in range(8):
@@ -260,7 +266,6 @@ def tile_archived_patch_probes_d1_kernel(
         def finish(i, a, part):
             if part == 2:
                 add_depth(i, a)
-                relu_depth(i, a)
             else:
                 finish_concepts(i, a, part)
 
@@ -275,11 +280,8 @@ def tile_archived_patch_probes_d1_kernel(
             "BM": scaled_bias,
             "M": multiply,
             "EP": finish,
+            "RL": relu_depth,
         }
-
-        for n in range(5):
-            spare = psum.tile([P, 512], F32, name="bank", tag="bank")
-            nc.tensor.matmul(spare[:], lhsT=warm[:, 0:P], rhs=warm[:], start=True, stop=True)
 
         for word in HEAD.split():
             kind, digits = word.split(":")
@@ -293,27 +295,25 @@ def tile_archived_patch_probes_d1_kernel(
                 steps[kind](*[int(n) for n in digits])
 
         for n, group in enumerate(GROUPS):
-            coming = [(i, g) for i in (GROUPS[n + 1] if n + 1 < len(GROUPS) else ()) for g in range(G)]
-            for i in group:
-                for g in range(G):
-                    turn_x(i, g)
-                    copy_out(("x", i, g), "s")
-            done = 0
-            on_vector = [key for key in coming if key[1] not in straight[key[0]]]
-            on_scalar = [key for key in coming if key[1] in straight[key[0]]]
-            for i in group:
-                for g in range(G):
-                    quantize_x(i, g)
-            for i in group:
-                for a in range(2):
-                    scaled_bias(i, a)
-                for a, part in ((0, 2), (1, 2), (0, 0), (0, 1), (1, 0), (1, 1)):
-                    multiply(i, a, part)
-                    finish(i, a, part)
-                    if part in (1, 2) and done < len(on_vector):
-                        widen_group(*on_vector[done])
-                        done += 1
-                for key in on_scalar[i - group[0] : i - group[0] + 1]:
-                    widen_group(*key)
-            for key in on_vector[done:] + on_scalar[len(group) :]:
-                widen_group(*key)
+            coming = [(i, g) for part in GROUPS[n + 2 : n + 3] for i in part for g in range(G)]
+            products = [(i, a, part) for i in group for a, part in TILE_ORDER]
+            turn_at = len(products) - len(TILE_ORDER)
+            for k, (i, a, part) in enumerate(products):
+                following = [(j, g) for later in GROUPS[n + 1 : n + 2] for j in later for g in range(G)]
+                if k == turn_at:
+                    for j, g in following:
+                        turn_x(j, g)
+                        copy_out(("x", j, g), "s")
+                if (a, part) == TILE_ORDER[0]:
+                    scaled_bias(i, 0)
+                    scaled_bias(i, 1)
+                multiply(i, a, part)
+                finish(i, a, part)
+                if part == 2:
+                    relu_depth(i, a)
+                if k == turn_at + 1:
+                    for j, g in following:
+                        quantize_x(j, g)
+                if part > 0 and coming:
+                    widen_group(*coming[0])
+                    coming = coming[1:]

from contextlib import ExitStack

import concourse.mybir as mybir
from concourse.masks import make_identity

T, K, C, D = 2048, 1536, 1024, 512
FLOPS = 2 * T * K * (C + D)

F32 = mybir.dt.float32
BF16 = mybir.dt.bfloat16
I32 = mybir.dt.int32
U32 = mybir.dt.uint32
U8 = mybir.dt.uint8
FP8 = mybir.dt.float8_e4m3fn
FP8X4 = mybir.dt.float8_e4m3fn_x4
FP4X4 = mybir.dt.float4_e2m1fn_x4
ADD = mybir.AluOpType.add
MULT = mybir.AluOpType.mult
COPY = mybir.ActivationFunctionType.Copy
RELU = mybir.ActivationFunctionType.Relu

P = 128
G = K // 512
TILES = T // P
PAIRS = TILES // 2
BLOCKS = K // 128
STRAIGHT = [(2,)] * 7 + [()]

HEAD = """
    WI:00 WI:02 WI:01 TX:00 BI:1 XX:00s BI:2 XB:1 TX:01 QX:00 TX:02 XX:01s
    TW:00 XX:02s WI:10 XB:2 TW:01 QX:01 WI:12 QX:02 TX:10 XW:01v BI:0 M:002
    WI:11 MC:0 XX:10s XW:00s QW:01 M:012 EP:002 XB:0 QW:00 TX:12 XW:02s QX:10
    WI:20 TX:11 BM:00 TW:10 EP:012 TW:11 XX:12s WI:21 XX:11s TW:20 QX:12 XW:11s
    QW:02 TW:21 QX:11 XW:12s WI:31 XW:10s TX:20 QW:12 M:112 BM:01 QW:11 QW:10
    WI:41 M:102 XW:20s XW:22v M:000 XX:20s EP:112 WI:22 M:110 EP:000 XW:21v M:010
    BM:11 EP:102 TX:21 QW:21 TX:22 BM:10 WI:40 TW:30 EP:110 XX:21s TW:31 QX:20
    XX:22s EP:010 M:100 XW:31s QX:21 QX:22 XW:32s QW:20 M:212 QW:31 XW:30s EP:100
    M:202 RL:00 WI:51 BM:20 M:210 QW:32 QW:30 QW:22 M:200 WI:32 EP:212 EP:202
    M:001 BM:21 WI:30 M:111 WI:61 RL:20 M:101 EP:001 RL:10 M:011 EP:210 WI:42
    EP:111 TX:32 EP:200 RL:21 TX:41 EP:101 TX:30 XX:32s TX:31 WI:50 TX:40 XX:30s
    TX:42 XX:31s EP:011 M:201 XX:40s QX:32 QX:30 XX:41s M:211 QX:31 WI:60 XX:42s
    WI:52 EP:201 EP:211 QX:40 RL:01 QX:41 QX:42 RL:11 WI:62
"""
TILE_ORDER = ((0, 2), (1, 2), (0, 0), (0, 1), (1, 0), (1, 1))
GROUPS = ((3, 4), (5, 6), (7,))


def tile_archived_patch_probes_d1_kernel(
    tc, x_bytes, x_scale, w, b, m, v_words, v_scales, c, concepts, depth
):
    nc = tc.nc

    x_rows = x_bytes.rearrange("(p i) k -> p i k", i=TILES)
    concept_rows = concepts.rearrange("(p i) n -> p i n", i=TILES)
    depth_rows = depth.rearrange("(p i) n -> p i n", i=TILES)

    with ExitStack() as ctx:
        keep = ctx.enter_context(tc.tile_pool(name="keep", bufs=1))
        work = ctx.enter_context(tc.tile_pool(name="work", bufs=4))
        psum = ctx.enter_context(tc.psum_pool(name="psum", bufs=8))
        ctx.enter_context(tc.manual_schedule())

        bias_row = keep.tile([P, C + D], BF16, name="bias_row")
        ones = keep.tile([P, P], BF16, name="ones")
        ident = keep.tile([P, P], F32, name="ident")
        bias = keep.tile([P, C + D], F32, name="bias")
        m_raw = keep.tile([P, TILES], BF16, name="m_raw")
        m_col = keep.tile([P, TILES], F32, name="m_col")
        x_sc = keep.tile([P, TILES * BLOCKS], F32, name="x_sc")
        v_code = keep.tile([P, G, 2 * D], U8, name="v_code", align_bytes=64)
        v_plane = keep.tile([P, G, D], U8, name="v_plane", align_bytes=64)
        w_in = [keep.tile([P, K], BF16, name="w_in%d" % j, tag="w_in%d" % j) for j in range(C // P)]
        x8 = [keep.tile([P, 2, K], U8, name="x8_%d" % i, tag="x8_%d" % i) for i in range(PAIRS)]
        w_code = [keep.tile([P, G, 512], U32, name="w_code%d" % h, tag="w_code%d" % h, align_bytes=64) for h in range(2)]
        w_plane = [keep.tile([P, G, 512], U8, name="w_plane%d" % h, tag="w_plane%d" % h, align_bytes=64) for h in range(2)]
        x_code = [keep.tile([P, G, 256], U32, name="x_code%d" % i, tag="x_code%d" % i, align_bytes=64) for i in range(PAIRS)]
        x_plane = [keep.tile([P, G, 256], U8, name="x_plane%d" % i, tag="x_plane%d" % i, align_bytes=64) for i in range(PAIRS)]

        def load_w(j):
            nc.sync.dma_start(out=w_in[j][:], in_=w[P * j : P * (j + 1), :])

        def load_x(i):
            nc.sync.dma_start(out=x8[i][:], in_=x_rows[:, 2 * i : 2 * i + 2, :])

        nc.vector.memset(bias_row[:], 0.0)
        make_identity(nc, ident[:])
        nc.vector.memset(ones[:], 1.0)
        nc.vector.memset(v_plane[:].rearrange("p g n -> p (g n)").bitcast(I32), 0)
        nc.scalar.dma_start(out=x_sc[:], in_=x_scale.rearrange("(p i) j -> p (i j)", i=TILES))
        load_x(0)
        load_w(0)
        nc.scalar.dma_start(out=bias_row[0:1, 0:C], in_=b.rearrange("(o n) -> o n", o=1))
        nc.scalar.dma_start(out=bias_row[0:1, C : C + D], in_=c.rearrange("(o n) -> o n", o=1))
        nc.scalar.dma_start(out=m_raw[:], in_=m.rearrange("(p i) -> p i", i=TILES))
        nc.sync.dma_start(out=v_code[:].bitcast(I32), in_=v_words.rearrange("g p n -> p g n").bitcast(I32))
        load_w(1)
        for q in range(4):
            nc.sync.dma_start(
                out=v_plane[32 * q : 32 * q + 4, :, :].bitcast(I32),
                in_=v_scales[:, 4 * q : 4 * q + 4, :].rearrange("g r n -> r g n").bitcast(I32),
            )
        load_x(1)
        load_w(2)
        load_w(3)
        load_w(4)
        load_x(2)
        load_w(5)
        load_w(6)
        load_w(7)
        for i in range(3, PAIRS):
            load_x(i)

        straight = STRAIGHT
        banks = {}
        grouped = {}
        wide = {}

        def spread_bias(s):
            cols = slice(512 * s, 512 * (s + 1))
            banks["b", s] = psum.tile([P, 512], F32, name="bank", tag="bank")
            nc.tensor.matmul(banks["b", s][:], lhsT=ones[:], rhs=bias_row[:, cols], start=True, stop=True)

        def copy_bias(s):
            nc.scalar.copy(out=bias[:, 512 * s : 512 * (s + 1)], in_=banks["b", s][:])

        def turn_w(jj, a):
            words = w_in[2 * jj + a][:].bitcast(F32)
            for g in range(G):
                if a == 0:
                    banks["w", jj, g] = psum.tile([P, 2, 256], F32, name="turned", tag="bank")
                for u in range(2):
                    nc.tensor.transpose(
                        banks["w", jj, g][:, u, P * a : P * (a + 1)],
                        words[:, 256 * g + u : 256 * (g + 1) : 2],
                        ident[:],
                    )

        def copy_out(key, engine):
            kind, i, g = key
            if (kind, i) not in grouped:
                grouped[kind, i] = work.tile([P, G, 1024], BF16, name="grouped", tag="grouped", align_bytes=64)
            out = grouped[kind, i][:, g, :].bitcast(F32).rearrange("p (r u) -> p r u", u=2)
            source = banks[key][:].rearrange("p u r -> p r u")
            if engine == "v":
                nc.vector.tensor_copy(out=out, in_=source)
            else:
                nc.scalar.copy(out=out, in_=source)

        def quantize_w(jj, g):
            h, cols = jj // 2, slice(256 * (jj % 2), 256 * (jj % 2) + 256)
            nc.vector.quantize_mx(
                out=w_code[h][:, g, cols].bitcast(FP8X4), scales=w_plane[h][:, g, cols], in_=grouped["w", jj][:, g, :]
            )

        def widen(i, a, j):
            if i not in wide:
                wide[i] = work.tile([P, 2, K], BF16, name="wide", tag="wide")
            g, q = divmod(j, 4)
            col = BLOCKS * (2 * i + a) + j
            if g in straight[i]:
                nc.scalar.activation(
                    out=wide[i][:, a, P * j : P * (j + 1)],
                    in_=x8[i][:, a, P * j : P * (j + 1)].bitcast(FP8),
                    func=COPY,
                    scale=x_sc[:, col : col + 1],
                )
                return
            out = wide[i][:, a, 512 * g : 512 * (g + 1)].rearrange("p (u s e) -> p s u e", u=2, e=2)
            nc.vector.tensor_scalar(
                out=out[:, 32 * q : 32 * (q + 1), :, :],
                in0=x8[i][:, a, P * j : P * (j + 1)].bitcast(FP8).rearrange("p (s u e) -> p s u e", u=2, e=2),
                scalar1=x_sc[:, col : col + 1],
                scalar2=None,
                op0=MULT,
            )

        def turn_x(i, g):
            bank = psum.tile([P, 2, 256], F32, name="turned", tag="bank")
            for a in range(2):
                words = wide[i][:, a, :].bitcast(F32)
                for u in range(2):
                    if g in straight[i]:
                        picked = words[:, 256 * g + u : 256 * (g + 1) : 2]
                    else:
                        picked = words[:, 256 * g + P * u : 256 * g + P * (u + 1)]
                    nc.tensor.transpose(bank[:, u, P * a : P * (a + 1)], picked, ident[:])
            banks["x", i, g] = bank

        def quantize_x(i, g):
            nc.vector.quantize_mx(
                out=x_code[i][:, g, :].bitcast(FP8X4), scales=x_plane[i][:, g, :], in_=grouped["x", i][:, g, :]
            )

        def pieces(i, a, part):
            if (i, a, part) == (PAIRS - 1, 1, 1):
                return [slice(0, 256), slice(256, 512)]
            return [slice(0, 512)]

        def multiply(i, a, part):
            tokens = slice(P * a, P * (a + 1))
            for cols in pieces(i, a, part):
                bank = psum.tile([P, 512], F32, name="bank", tag="bank")
                for g in range(G):
                    if part == 2:
                        rhs, rhs_scale = v_code[:, g, :].bitcast(FP4X4), v_plane[:, g, :]
                    else:
                        rhs, rhs_scale = w_code[part][:, g, cols].bitcast(FP8X4), w_plane[part][:, g, cols]
                    nc.tensor.matmul_mx(
                        out=bank[:, cols],
                        lhsT=x_code[i][:, g, tokens].bitcast(FP8X4),
                        lhsT_scale=x_plane[i][:, g, tokens],
                        rhs=rhs,
                        rhs_scale=rhs_scale,
                        start=(g == 0),
                        stop=(g == G - 1),
                    )
                banks["m", i, a, part, cols.start] = bank

        complete = set()
        con = {}
        dep = {}

        def scaled_bias(i, a):
            if i not in con:
                con[i] = work.tile([P, 2, C], F32, name="con", tag="con")
            t = 2 * i + a
            nc.scalar.activation(out=con[i][:, a, :], in_=bias[:, 0:C], func=COPY, scale=m_col[:, t : t + 1])

        def finish_concepts(i, a, h):
            t = 2 * i + a
            for cols in pieces(i, a, h):
                both = slice(512 * h + cols.start, 512 * h + cols.stop)
                place = con[i][:, a, both]
                nc.vector.scalar_tensor_tensor(
                    out=place,
                    in0=banks["m", i, a, h, cols.start][:, cols],
                    scalar=m_col[:, t : t + 1],
                    in1=place,
                    op0=MULT,
                    op1=ADD,
                )
                if i == PAIRS - 1:
                    nc.sync.dma_start(out=concept_rows[:, t, both], in_=place)
            complete.add((i, a, h))
            if (i, a, 1 - h) in complete and i < PAIRS - 1:
                nc.sync.dma_start(out=concept_rows[:, t, :], in_=con[i][:, a, :])

        def add_depth(i, a):
            if i not in dep:
                dep[i] = work.tile([P, 2, D], F32, name="dep", tag="dep")
            nc.vector.tensor_tensor(out=dep[i][:, a, :], in0=banks["m", i, a, 2, 0][:], in1=bias[:, C : C + D], op=ADD)

        def relu_depth(i, a):
            place = dep[i][:, a, :]
            nc.scalar.activation(out=place, in_=place, func=RELU)
            complete.add((i, a))
            if i == PAIRS - 1:
                nc.sync.dma_start(out=depth_rows[:, 2 * i + a, :], in_=place)
            elif (i, 1 - a) in complete:
                nc.sync.dma_start(out=depth_rows[:, 2 * i : 2 * i + 2, :], in_=dep[i][:])

        def widen_group(i, g):
            for n in range(8):
                widen(i, n // 4, 4 * g + n % 4)

        def finish(i, a, part):
            if part == 2:
                add_depth(i, a)
            else:
                finish_concepts(i, a, part)

        steps = {
            "TW": turn_w,
            "QW": quantize_w,
            "BI": spread_bias,
            "XB": copy_bias,
            "WI": widen_group,
            "TX": turn_x,
            "QX": quantize_x,
            "BM": scaled_bias,
            "M": multiply,
            "EP": finish,
            "RL": relu_depth,
        }

        for word in HEAD.split():
            kind, digits = word.split(":")
            if kind == "MC":
                nc.vector.tensor_copy(out=m_col[:], in_=m_raw[:])
            elif kind == "XW":
                copy_out(("w", int(digits[0]), int(digits[1])), digits[2])
            elif kind == "XX":
                copy_out(("x", int(digits[0]), int(digits[1])), digits[2])
            else:
                steps[kind](*[int(n) for n in digits])

        for n, group in enumerate(GROUPS):
            coming = [(i, g) for part in GROUPS[n + 2 : n + 3] for i in part for g in range(G)]
            products = [(i, a, part) for i in group for a, part in TILE_ORDER]
            turn_at = len(products) - len(TILE_ORDER)
            for k, (i, a, part) in enumerate(products):
                following = [(j, g) for later in GROUPS[n + 1 : n + 2] for j in later for g in range(G)]
                if k == turn_at:
                    for j, g in following:
                        turn_x(j, g)
                        copy_out(("x", j, g), "s")
                if (a, part) == TILE_ORDER[0]:
                    scaled_bias(i, 0)
                    scaled_bias(i, 1)
                multiply(i, a, part)
                finish(i, a, part)
                if part == 2:
                    relu_depth(i, a)
                if k == turn_at + 1:
                    for j, g in following:
                        quantize_x(j, g)
                if part > 0 and coming:
                    widen_group(*coming[0])
                    coming = coming[1:]
